import numpy as np
import ml_dtypes


def mxq(x, axis, fmt="e4m3"):
    dtype, down = {"e4m3": (ml_dtypes.float8_e4m3fn, 7), "e5m2": (ml_dtypes.float8_e5m2, 14)}[fmt]
    v = np.moveaxis(np.asarray(x, np.float32).astype(ml_dtypes.bfloat16).astype(np.float64), axis, -1)
    blocks = v.reshape(v.shape[:-1] + (-1, 32))
    amax = np.abs(blocks).max(-1, keepdims=True)
    byte = np.maximum(np.where(amax > 0, np.frexp(amax)[1] - 1 + 127, 0) - down, 1)
    scale = np.exp2(byte - 127.0)
    codes = (blocks / scale).astype(np.float32).astype(dtype).astype(np.float64)
    return np.moveaxis((codes * scale).reshape(v.shape), -1, axis)


WIDE = False


def mx_kscale(k):
    if not WIDE:
        return np.ones(k)
    levels = np.array([10, -10, 5, -5, 0])
    if k % 512:
        return np.exp2(np.random.permutation(np.resize(levels, k // 32))).repeat(32)
    a = np.empty((k // 512, 16))
    for p in range(k // 512):
        a[p, :8] = np.random.permutation(np.resize(levels, 8))
        for g in range(8):
            far = levels[np.abs(levels - a[p, g]) >= 10]
            a[p, g + 8] = far[np.random.randint(len(far))]
    return np.exp2(a.ravel()).repeat(32)


def f64(x):
    return np.asarray(x).astype(np.float64)


def striped(idx):
    return np.tile(idx.reshape(-1, 16).T, (8, 1)).astype(np.uint16)


def unstriped(offs):
    return offs[:16].T.reshape(-1).astype(np.int64)


def pack_weight(w):
    k, n = w.shape
    w = f64(np.asarray(w, np.float32).astype(ml_dtypes.bfloat16)).reshape(k // 32, 32, n)
    amax = np.abs(w).max(1)
    byte = np.clip(np.where(amax > 0, np.frexp(amax)[1] - 1 + 127 - 7, 1), 1, 254)
    scaled = (w * np.exp2(127.0 - byte)[:, None, :]).reshape(k, n).astype(np.float32)
    words = np.ascontiguousarray(scaled.reshape(k // 512, 128, 4, n).transpose(0, 1, 3, 2)).astype(ml_dtypes.float8_e4m3fn).view(np.uint8)
    return words, np.ascontiguousarray(byte.astype(np.uint8).reshape(k // 512, 16, n))


def unpack_weight(words, scales):
    g, p, n, _ = words.shape
    vals = np.ascontiguousarray(words).view(ml_dtypes.float8_e4m3fn).astype(np.float64) * np.repeat(np.exp2(scales.astype(np.float64) - 127.0), 8, axis=1)[..., None]
    return vals.transpose(0, 1, 3, 2).reshape(g * 512, n)


K, T, S, D, N = 1024, 2048, 1024, 4, 256
P = 2 ** 7


def setup_inputs():
    n = np.random.standard_normal
    s = mx_kscale(K)[:, None]
    packed_xT = pack_weight(n((K, T)) * s)
    return {
        "x_words": packed_xT[0],
        "x_scales": packed_xT[1],
        "w1": (n((K, N)) / np.sqrt(K) / s).astype(np.float32),
        "cnt": (np.tile(np.floor(np.random.uniform(0.0, 20.0, S)), (P, 1))).astype(np.float32),
        "qv": (np.random.uniform(-1.0, 1.0, (N, S))).astype(np.float32),
        "offs": striped(np.random.permutation(T)[:S]),
    }


def reference(x_words, x_scales, w1, cnt, qv, offs):
    xq = unpack_weight(x_words, x_scales)[:, unstriped(offs)]
    y = mxq(f64(w1), 0, "e4m3").T @ xq
    top = y.reshape(len(y), -1, D).max(axis=2)
    ex = np.exp(y - np.repeat(top, D, axis=1))
    total = ex.reshape(len(ex), -1, D).sum(axis=2)
    pri = ex / np.repeat(total, D, axis=1)
    mc = f64(cnt)[:1].reshape(len(f64(cnt)[:1]), -1, D).max(axis=2)
    sig = np.log(pri) + (np.repeat(0.03 * (mc + 50.0), D, axis=1)) * f64(qv)
    es = np.exp(sig)
    ts = es.reshape(len(es), -1, D).sum(axis=2)
    tc = f64(cnt)[:1].reshape(len(f64(cnt)[:1]), -1, D).sum(axis=2) + 1.0
    return np.exp(sig) / np.repeat(ts, D, axis=1) - (f64(cnt)[:1] / np.repeat(tc, D, axis=1))

@@ -1,0 +1,281 @@
+import math
+from contextlib import ExitStack
+
+import concourse.mybir as mybir
+from concourse.masks import make_identity
+
+K, T, S, D, N = 1024, 2048, 1024, 4, 256
+FLOPS = 2 * K * S * N
+
+F32 = mybir.dt.float32
+BF16 = mybir.dt.bfloat16
+I32 = mybir.dt.int32
+U32 = mybir.dt.uint32
+U16 = mybir.dt.uint16
+U8 = mybir.dt.uint8
+FP8X4 = mybir.dt.float8_e4m3fn_x4
+ALU = mybir.AluOpType
+ACT = mybir.ActivationFunctionType
+AXIS_X = mybir.AxisListType.X
+
+P = 128
+PASSES = K // 512
+HALF = 512
+GROUPS = HALF // D
+
+GUESS_RATE, GUESS_BIAS, GUESS_SHIFT = 0.476, 1.057, -1.8014
+QUART_SCALE = math.sqrt(0.5)
+QUART_BIAS = -1.0 / (12.0 * QUART_SCALE**3)
+QUAD_SCALE = math.sqrt(1.0 / 3.0)
+QUAD_BIAS = -13.0 / (27.0 * QUAD_SCALE)
+LOG_SHIFT = GUESS_SHIFT - QUART_BIAS**4 - QUAD_BIAS**2
+
+ENG_I = ["g", "v", "g", "g"]
+ENG_C = ["v", "v", "g", "v"]
+ENG_H = ["g", "g", "v", "v"]
+PATH = ["log", "log", "log", "dir"]
+LOADS = ["s0", "s1", "s2", "s3", "x0", "x1", "w0", "w1", "q0", "q1", "q2", "q3"]
+PIECES = [1, 1, 2, 2]
+
+
+def tile_picked_ypuct_gum_p_kernel(tc, x_words, x_scales, w1, cnt, qv, offs, out):
+    nc = tc.nc
+    engines = {"v": nc.vector, "g": nc.gpsimd}
+    with ExitStack() as ctx:
+        keep = ctx.enter_context(tc.tile_pool(name="keep", bufs=1))
+        psum = ctx.enter_context(tc.psum_pool(name="psum", bufs=1))
+
+        planes = keep.tile([P, T], U8, name="planes", align_bytes=64)
+        nc.gpsimd.memset(planes[:].bitcast(I32), 0)
+        offsets = keep.tile([P, S // 16], U16, name="offsets")
+        nc.sync.dma_start(offsets[:], offs)
+        visits = keep.tile([P, 2, D], F32, name="visits")
+        nc.sync.dma_start(visits[:], cnt[0:1, :].rearrange("o (h p d) -> p (o h) d", h=2, d=D))
+
+        chunks = [(mt, h) for h in range(S // HALF) for mt in range(N // P)]
+        q_tiles, words, w_raw = {}, {}, {}
+        for what in LOADS:
+            i = int(what[1])
+            if what[0] == "s":
+                nc.sync.dma_start(
+                    planes[32 * i : 32 * i + 4 * PASSES, :].bitcast(I32),
+                    x_scales[:, 4 * i : 4 * i + 4, :].bitcast(I32),
+                )
+            elif what[0] == "q":
+                mt, h = chunks[i]
+                q = keep.tile([P, HALF], F32, name=f"q{i}")
+                nc.sync.dma_start(q[:], qv[P * mt : P * (mt + 1), HALF * h : HALF * (h + 1)])
+                q_tiles[i] = q
+            elif what[0] == "x":
+                table = keep.tile([P, T], I32, name=f"words{i}", align_bytes=64)
+                nc.sync.dma_start(table[:], x_words[i].rearrange("p n t -> p (n t)").bitcast(I32))
+                words[i] = table
+            else:
+                raw = keep.tile([P, 4, N], F32, name=f"w_raw{i}")
+                nc.sync.dma_start(raw[:], w1[512 * i : 512 * (i + 1), :].rearrange("(p t) n -> p t n", t=4))
+                w_raw[i] = raw
+
+        ident = keep.tile([P, P], F32, name="ident")
+        make_identity(nc, ident[:])
+
+        most = keep.tile([P, 2], F32, name="most")
+        nc.vector.tensor_reduce(most[:], visits[:], AXIS_X, ALU.max)
+        total = keep.tile([P, 2], F32, name="total")
+        padded = keep.tile([P, 2, D], F32, name="padded")
+        for h in range(2):
+            nc.scalar.activation(
+                padded[:, h, :], visits[:, h, :], ACT.Identity, bias=1.0 / D, accum_out=total[:, h : h + 1]
+            )
+        inv_total = keep.tile([P, 2], F32, name="inv_total")
+        nc.vector.reciprocal(inv_total[:], total[:])
+        share_col = keep.tile([P, 2, D], F32, name="share_col")
+        for h in range(2):
+            nc.scalar.activation(share_col[:, h, :], visits[:, h, :], ACT.Copy, scale=inv_total[:, h : h + 1])
+
+        weight = keep.tile([P, S // D], F32, name="weight")
+        weight_col = keep.tile([P, 2], F32, name="weight_col")
+        nc.scalar.activation(weight_col[:], most[:], ACT.Identity, bias=0.03 * 50.0, scale=0.03)
+        weight_ps = psum.tile([P, 2 * P], F32, name="weight_ps")
+        for h in range(2):
+            nc.tensor.transpose(
+                weight_ps[:, P * h : P * (h + 1)], weight_col[:, h : h + 1].to_broadcast([P, P]), ident[:]
+            )
+        nc.scalar.copy(weight[:], weight_ps[:])
+        share = keep.tile([P, S], F32, name="share")
+        share_ps = {}
+        for h in range(2):
+            if h == 0:
+                spread = psum.tile([P, HALF], F32, name="spread_s0", tag="wide", bufs=2)
+            else:
+                spread = psum.tile([P, HALF], F32, name="spread_s1")
+            share_ps[h] = spread
+            for d in range(D):
+                nc.tensor.transpose(
+                    spread[:, P * d : P * (d + 1)], share_col[:, h, d : d + 1].to_broadcast([P, P]), ident[:]
+                )
+            if any(ENG_H[i] == "g" and chunks[i][1] == h for i in range(len(chunks))):
+              nc.scalar.copy(
+                share[:, HALF * h : HALF * (h + 1)].rearrange("p (v d) -> p v d", d=D),
+                spread[:].rearrange("p (d v) -> p v d", d=D),
+            )
+
+        picked_planes = keep.tile([P, S], U8, name="picked_planes", align_bytes=64)
+        nc.vector.tensor_copy(picked_planes[:], planes[:].indirect(offsets[:]))
+        picked0 = keep.tile([P, S], U32, name="picked0", align_bytes=64)
+        nc.vector.tensor_copy(picked0[:], words[0][:].bitcast(U32).indirect(offsets[:]))
+        picked = {(0, h): picked0[:, HALF * h : HALF * (h + 1)] for h in range(2)}
+
+        def gather_last(h):
+            tile = keep.tile([P, HALF], U32, name=f"picked1_{h}", align_bytes=64)
+            cols = HALF // 16
+            nc.vector.tensor_copy(
+                tile[:], words[1][:].bitcast(U32).indirect(offsets[:, cols * h : cols * (h + 1)])
+            )
+            picked[(1, h)] = tile[:]
+
+        w_codes, w_scales = {}, {}
+
+        def quantise(g, mt):
+            grouped = keep.tile([P, P, 4], BF16, name=f"w_bf{g}{mt}", align_bytes=64)
+            nc.scalar.copy(
+                grouped[:].rearrange("p (c i) t -> p c t i", i=4),
+                w_raw[g][:, :, P * mt : P * (mt + 1)].rearrange("p t (c i) -> p c t i", i=4),
+            )
+            codes = keep.tile([P, P], U32, name=f"w_codes{g}{mt}", align_bytes=64)
+            scales = keep.tile([P, P], U8, name=f"w_scales{g}{mt}", align_bytes=64)
+            nc.vector.quantize_mx(
+                out=codes[:].bitcast(FP8X4), scales=scales[:], in_=grouped[:].rearrange("p m t -> p (m t)")
+            )
+            w_codes[(g, mt)], w_scales[(g, mt)] = codes, scales
+
+        gather_last(0)
+        quantise(0, 0)
+        quantise(0, 1)
+        quantise(1, 0)
+        quantise(1, 1)
+        gather_last(1)
+
+        def by_group(ap):
+            return ap.rearrange("p (v d) -> p v d", d=D)
+
+        def per_group(ap):
+            return ap.unsqueeze(2).to_broadcast([P, ap.shape[1], D])
+
+        weighted, shifted, sums, logs = {}, {}, {}, {}
+
+        def weigh(i):
+            mt, h = chunks[i]
+            tile = keep.tile([P, HALF], F32, name=f"weighted{i}")
+            engines[ENG_I[i]].tensor_tensor(
+                by_group(tile[:]), by_group(q_tiles[i][:]),
+                per_group((weight if ENG_I[i] == "g" else weight_ps)[:, GROUPS * h : GROUPS * (h + 1)]), ALU.mult,
+            )
+            weighted[i] = tile
+
+        def front(i):
+            mt, h = chunks[i]
+            cols = slice(HALF * h, HALF * (h + 1))
+            y = psum.tile([P, HALF], F32, name=f"y{i}", tag="wide", bufs=2)
+            order = list(range(PASSES)) if mt == 0 else list(reversed(range(PASSES)))
+            for g in order:
+                nc.tensor.matmul_mx(
+                    out=y[:],
+                    lhsT=w_codes[(g, mt)][:].bitcast(FP8X4),
+                    lhsT_scale=w_scales[(g, mt)][:],
+                    rhs=picked[(g, h)].bitcast(FP8X4),
+                    rhs_scale=picked_planes[4 * g : P, cols],
+                    start=(g == order[0]),
+                    stop=(g == order[-1]),
+                )
+            z = keep.tile([P, HALF], F32, name=f"z{i}")
+            nc.vector.tensor_tensor(z[:], y[:], weighted[i][:], ALU.add)
+            top = keep.tile([P, GROUPS], F32, name=f"top{i}")
+            nc.vector.tensor_reduce(top[:], by_group(z[:]), AXIS_X, ALU.max)
+            low = keep.tile([P, HALF], F32, name=f"low{i}")
+            engines[ENG_C[i]].tensor_tensor(by_group(low[:]), by_group(z[:]), per_group(top[:]), ALU.subtract)
+            shifted[i] = low
+
+        def group_sums(i):
+            dealt = keep.tile([P, D, GROUPS], F32, name=f"dealt{i}")
+            nc.scalar.activation(dealt[:].rearrange("p d v -> p v d"), by_group(shifted[i][:]), ACT.Exp)
+            ts = psum.tile([P, P], F32, name=f"ts{i}", tag="sums", bufs=2)
+            for d in range(D):
+                nc.tensor.matmul(
+                    ts[:], dealt[:, d, :], ident[:], start=(d == 0), stop=(d == D - 1), is_transpose=True
+                )
+            sums[i] = ts
+
+        def middle(i):
+            ts = sums[i]
+            guess = keep.tile([P, P], F32, name=f"guess{i}")
+            nc.scalar.activation(guess[:], ts[:], ACT.Exp, bias=GUESS_BIAS, scale=-GUESS_RATE)
+            inverse = keep.tile([P, P], F32, name=f"inverse{i}")
+            nc.scalar.activation(inverse[:], guess[:], ACT.Exp, bias=GUESS_SHIFT)
+            near_one = keep.tile([P, P], F32, name=f"near_one{i}")
+            nc.vector.tensor_tensor(near_one[:], ts[:], inverse[:], ALU.mult)
+            root = keep.tile([P, P], F32, name=f"root{i}")
+            nc.scalar.activation(root[:], near_one[:], ACT.Square, bias=QUART_BIAS - QUART_SCALE, scale=QUART_SCALE)
+            quad = keep.tile([P, P], F32, name=f"quad{i}")
+            nc.scalar.activation(quad[:], near_one[:], ACT.Square, bias=QUAD_BIAS - QUAD_SCALE, scale=QUAD_SCALE)
+            quart = keep.tile([P, P], F32, name=f"quart{i}")
+            nc.scalar.activation(quart[:], root[:], ACT.Square)
+            neg_log = psum.tile([P, P], F32, name=f"neg_log{i}", tag="logs", bufs=2)
+            terms = (guess, quad, quart)
+            for j, term in enumerate(terms):
+                nc.tensor.matmul(
+                    neg_log[:], term[:], ident[:], start=(j == 0), stop=(j == len(terms) - 1), is_transpose=True
+                )
+            logs[i] = neg_log
+
+        def finish(i, prob, lo, hi, tag):
+            mt, h = chunks[i]
+            result = keep.tile([P, hi - lo], F32, name=f"result{tag}")
+            cols = slice(HALF * h + lo, HALF * h + hi)
+            if ENG_H[i] == "g":
+                nc.gpsimd.tensor_tensor(result[:], prob[:], share[:, cols], ALU.subtract)
+            else:
+                nc.vector.tensor_tensor(
+                    by_group(result[:]), by_group(prob[:]),
+                    share_ps[h][:].rearrange("p (d v) -> p v d", d=D)[:, lo // D : hi // D, :], ALU.subtract,
+                )
+            nc.sync.dma_start(out[P * mt : P * (mt + 1), cols], result[:])
+
+        def back(i):
+            width = HALF // PIECES[i]
+            for j in range(PIECES[i]):
+                lo, hi = width * j, width * (j + 1)
+                logp = keep.tile([P, width], F32, name=f"logp{i}_{j}")
+                nc.vector.tensor_tensor(
+                    by_group(logp[:]), by_group(shifted[i][:, lo:hi]), per_group(logs[i][:, lo // D : hi // D]), ALU.add
+                )
+                prob = keep.tile([P, width], F32, name=f"prob{i}_{j}")
+                nc.scalar.activation(prob[:], logp[:], ACT.Exp, bias=LOG_SHIFT)
+                finish(i, prob, lo, hi, f"{i}_{j}")
+
+        def direct(i):
+            width = HALF // PIECES[i]
+            for j in range(PIECES[i]):
+                lo, hi = width * j, width * (j + 1)
+                ex = keep.tile([P, width], F32, name=f"ex{i}_{j}")
+                nc.scalar.activation(ex[:], shifted[i][:, lo:hi], ACT.Exp)
+                ts = keep.tile([P, width // D], F32, name=f"sum{i}_{j}")
+                nc.vector.tensor_reduce(ts[:], by_group(ex[:]), AXIS_X, ALU.add)
+                inv = keep.tile([P, width // D], F32, name=f"inv{i}_{j}")
+                nc.vector.reciprocal(inv[:], ts[:])
+                prob = keep.tile([P, width], F32, name=f"prob{i}_{j}")
+                nc.vector.tensor_tensor(by_group(prob[:]), by_group(ex[:]), per_group(inv[:]), ALU.mult)
+                finish(i, prob, lo, hi, f"{i}_{j}")
+
+        for i in range(len(chunks)):
+            weigh(i)
+        for step in range(len(chunks) + 2):
+            if 0 <= step - 2 < len(chunks) and PATH[step - 2] == "log":
+                back(step - 2)
+            if 0 <= step - 1 < len(chunks) and PATH[step - 1] == "log":
+                middle(step - 1)
+            if step < len(chunks):
+                front(step)
+                if PATH[step] == "log":
+                    group_sums(step)
+                else:
+                    direct(step)

@@ -30,11 +30,13 @@ QUAD_SCALE = math.sqrt(1.0 / 3.0)
 QUAD_BIAS = -13.0 / (27.0 * QUAD_SCALE)
 LOG_SHIFT = GUESS_SHIFT - QUART_BIAS**4 - QUAD_BIAS**2
 
-ENG_I = ["g", "v", "g", "g"]
-ENG_C = ["v", "v", "g", "v"]
-ENG_H = ["g", "g", "v", "v"]
+ENG_I = ["v", "v", "g", "g"]
+ENG_C = ["v", "v", "v", "v"]
+ENG_H = ["g", "v", "v", "v"]
+HOLD = (1, 1)
+ENG_M = ["","","",""]
 PATH = ["log", "log", "log", "dir"]
-LOADS = ["s0", "s1", "s2", "s3", "x0", "x1", "w0", "w1", "q0", "q1", "q2", "q3"]
+LOADS = ["c0", "s0", "s1", "s2", "s3", "x0", "x1", "w0", "w1", "q0", "q1", "q2", "q3"]
 PIECES = [1, 1, 2, 2]
 
 
@@ -50,13 +52,21 @@ def tile_picked_ypuct_gum_p_kernel(tc, x_words, x_scales, w1, cnt, qv, offs, out
         offsets = keep.tile([P, S // 16], U16, name="offsets")
         nc.sync.dma_start(offsets[:], offs)
         visits = keep.tile([P, 2, D], F32, name="visits")
-        nc.sync.dma_start(visits[:], cnt[0:1, :].rearrange("o (h p d) -> p (o h) d", h=2, d=D))
 
         chunks = [(mt, h) for h in range(S // HALF) for mt in range(N // P)]
         q_tiles, words, w_raw = {}, {}, {}
         for what in LOADS:
             i = int(what[1])
-            if what[0] == "s":
+            if what[0] == "c":
+                nc.sync.dma_start(visits[:], cnt[0:1, :].rearrange("o (h p d) -> p (o h) d", h=2, d=D))
+            elif what[0] == "u":
+                g, mt = i // 2, i % 2
+                part = keep.tile([P, 4, P], F32, name=f"w_part{i}")
+                nc.sync.dma_start(
+                    part[:], w1[512 * g : 512 * (g + 1), P * mt : P * (mt + 1)].rearrange("(p t) n -> p t n", t=4)
+                )
+                w_raw[(g, mt)] = part[:]
+            elif what[0] == "s":
                 nc.sync.dma_start(
                     planes[32 * i : 32 * i + 4 * PASSES, :].bitcast(I32),
                     x_scales[:, 4 * i : 4 * i + 4, :].bitcast(I32),
@@ -73,7 +83,8 @@ def tile_picked_ypuct_gum_p_kernel(tc, x_words, x_scales, w1, cnt, qv, offs, out
             else:
                 raw = keep.tile([P, 4, N], F32, name=f"w_raw{i}")
                 nc.sync.dma_start(raw[:], w1[512 * i : 512 * (i + 1), :].rearrange("(p t) n -> p t n", t=4))
-                w_raw[i] = raw
+                for mt in range(2):
+                    w_raw[(i, mt)] = raw[:, :, P * mt : P * (mt + 1)]
 
         ident = keep.tile([P, P], F32, name="ident")
         make_identity(nc, ident[:])
@@ -92,7 +103,7 @@ def tile_picked_ypuct_gum_p_kernel(tc, x_words, x_scales, w1, cnt, qv, offs, out
         for h in range(2):
             nc.scalar.activation(share_col[:, h, :], visits[:, h, :], ACT.Copy, scale=inv_total[:, h : h + 1])
 
-        weight = keep.tile([P, S // D], F32, name="weight")
+        weight = keep.tile([P, S], F32, name="weight")
         weight_col = keep.tile([P, 2], F32, name="weight_col")
         nc.scalar.activation(weight_col[:], most[:], ACT.Identity, bias=0.03 * 50.0, scale=0.03)
         weight_ps = psum.tile([P, 2 * P], F32, name="weight_ps")
@@ -100,7 +111,12 @@ def tile_picked_ypuct_gum_p_kernel(tc, x_words, x_scales, w1, cnt, qv, offs, out
             nc.tensor.transpose(
                 weight_ps[:, P * h : P * (h + 1)], weight_col[:, h : h + 1].to_broadcast([P, P]), ident[:]
             )
-        nc.scalar.copy(weight[:], weight_ps[:])
+        for h in range(2):
+            if any(ENG_I[i] == "g" and chunks[i][1] == h for i in range(len(chunks))):
+                nc.scalar.copy(
+                    weight[:, HALF * h : HALF * (h + 1)].rearrange("p (v d) -> p v d", d=D),
+                    weight_ps[:, P * h : P * (h + 1)].unsqueeze(2).to_broadcast([P, P, D]),
+                )
         share = keep.tile([P, S], F32, name="share")
         share_ps = {}
         for h in range(2):
@@ -113,7 +129,7 @@ def tile_picked_ypuct_gum_p_kernel(tc, x_words, x_scales, w1, cnt, qv, offs, out
                 nc.tensor.transpose(
                     spread[:, P * d : P * (d + 1)], share_col[:, h, d : d + 1].to_broadcast([P, P]), ident[:]
                 )
-            if any(ENG_H[i] == "g" and chunks[i][1] == h for i in range(len(chunks))):
+            if h == 0 or any(ENG_H[i] == "g" and chunks[i][1] == h for i in range(len(chunks))):
               nc.scalar.copy(
                 share[:, HALF * h : HALF * (h + 1)].rearrange("p (v d) -> p v d", d=D),
                 spread[:].rearrange("p (d v) -> p v d", d=D),
@@ -136,10 +152,12 @@ def tile_picked_ypuct_gum_p_kernel(tc, x_words, x_scales, w1, cnt, qv, offs, out
         w_codes, w_scales = {}, {}
 
         def quantise(g, mt):
-            grouped = keep.tile([P, P, 4], BF16, name=f"w_bf{g}{mt}", align_bytes=64)
+            grouped = keep.tile(
+                [P, P, 4], BF16, name=f"w_bf{g}{mt}", tag="handover" if (g, mt) == HOLD else f"w_bf{g}{mt}", align_bytes=64
+            )
             nc.scalar.copy(
                 grouped[:].rearrange("p (c i) t -> p c t i", i=4),
-                w_raw[g][:, :, P * mt : P * (mt + 1)].rearrange("p t (c i) -> p c t i", i=4),
+                w_raw[(g, mt)].rearrange("p t (c i) -> p c t i", i=4),
             )
             codes = keep.tile([P, P], U32, name=f"w_codes{g}{mt}", align_bytes=64)
             scales = keep.tile([P, P], U8, name=f"w_scales{g}{mt}", align_bytes=64)
@@ -161,15 +179,22 @@ def tile_picked_ypuct_gum_p_kernel(tc, x_words, x_scales, w1, cnt, qv, offs, out
         def per_group(ap):
             return ap.unsqueeze(2).to_broadcast([P, ap.shape[1], D])
 
-        weighted, shifted, sums, logs = {}, {}, {}, {}
+        weighted, shifted, sums, logs, plain = {}, {}, {}, {}, {}
+        late = keep.tile([P, HALF * max(1, len([e for e in ENG_I if e == "g"]))], F32, name="late", tag="handover", align_bytes=64)
 
         def weigh(i):
             mt, h = chunks[i]
-            tile = keep.tile([P, HALF], F32, name=f"weighted{i}")
-            engines[ENG_I[i]].tensor_tensor(
-                by_group(tile[:]), by_group(q_tiles[i][:]),
-                per_group((weight if ENG_I[i] == "g" else weight_ps)[:, GROUPS * h : GROUPS * (h + 1)]), ALU.mult,
-            )
+            if ENG_I[i] == "g":
+                slot = len([e for e in ENG_I[:i] if e == "g"])
+                tile = late[:, HALF * slot : HALF * (slot + 1)]
+                nc.gpsimd.tensor_tensor(tile, q_tiles[i][:], weight[:, HALF * h : HALF * (h + 1)], ALU.mult)
+            else:
+                whole = keep.tile([P, HALF], F32, name=f"weighted{i}")
+                tile = whole[:]
+                nc.vector.tensor_tensor(
+                    by_group(tile), by_group(q_tiles[i][:]),
+                    per_group(weight_ps[:, GROUPS * h : GROUPS * (h + 1)]), ALU.mult,
+                )
             weighted[i] = tile
 
         def front(i):
@@ -188,7 +213,7 @@ def tile_picked_ypuct_gum_p_kernel(tc, x_words, x_scales, w1, cnt, qv, offs, out
                     stop=(g == order[-1]),
                 )
             z = keep.tile([P, HALF], F32, name=f"z{i}")
-            nc.vector.tensor_tensor(z[:], y[:], weighted[i][:], ALU.add)
+            nc.vector.tensor_tensor(z[:], y[:], weighted[i], ALU.add)
             top = keep.tile([P, GROUPS], F32, name=f"top{i}")
             nc.vector.tensor_reduce(top[:], by_group(z[:]), AXIS_X, ALU.max)
             low = keep.tile([P, HALF], F32, name=f"low{i}")
@@ -226,13 +251,17 @@ def tile_picked_ypuct_gum_p_kernel(tc, x_words, x_scales, w1, cnt, qv, offs, out
                     neg_log[:], term[:], ident[:], start=(j == 0), stop=(j == len(terms) - 1), is_transpose=True
                 )
             logs[i] = neg_log
+            if ENG_M[i] != "":
+                ex = keep.tile([P, HALF], F32, name=f"ex{i}")
+                nc.scalar.activation(ex[:], shifted[i][:], ACT.Exp)
+                plain[i] = ex
 
         def finish(i, prob, lo, hi, tag):
             mt, h = chunks[i]
             result = keep.tile([P, hi - lo], F32, name=f"result{tag}")
             cols = slice(HALF * h + lo, HALF * h + hi)
-            if ENG_H[i] == "g":
-                nc.gpsimd.tensor_tensor(result[:], prob[:], share[:, cols], ALU.subtract)
+            if ENG_H[i] == "g" or h == 0:
+                engines[ENG_H[i]].tensor_tensor(result[:], prob[:], share[:, cols], ALU.subtract)
             else:
                 nc.vector.tensor_tensor(
                     by_group(result[:]), by_group(prob[:]),
@@ -240,7 +269,21 @@ def tile_picked_ypuct_gum_p_kernel(tc, x_words, x_scales, w1, cnt, qv, offs, out
                 )
             nc.sync.dma_start(out[P * mt : P * (mt + 1), cols], result[:])
 
+        def back_mul(i):
+            inv = keep.tile([P, P], F32, name=f"inv{i}")
+            nc.scalar.activation(inv[:], logs[i][:], ACT.Exp, bias=LOG_SHIFT)
+            width = HALF // PIECES[i]
+            for j in range(PIECES[i]):
+                lo, hi = width * j, width * (j + 1)
+                prob = keep.tile([P, width], F32, name=f"prob{i}_{j}")
+                engines[ENG_M[i]].tensor_tensor(
+                    by_group(prob[:]), by_group(plain[i][:, lo:hi]), per_group(inv[:, lo // D : hi // D]), ALU.mult
+                )
+                finish(i, prob, lo, hi, f"{i}_{j}")
+
         def back(i):
+            if ENG_M[i] != "":
+                return back_mul(i)
             width = HALF // PIECES[i]
             for j in range(PIECES[i]):
                 lo, hi = width * j, width * (j + 1)
@@ -250,6 +293,23 @@ def tile_picked_ypuct_gum_p_kernel(tc, x_words, x_scales, w1, cnt, qv, offs, out
                 )
                 prob = keep.tile([P, width], F32, name=f"prob{i}_{j}")
                 nc.scalar.activation(prob[:], logp[:], ACT.Exp, bias=LOG_SHIFT)
+                finish(i, prob, lo, hi, f"{i}_{j}")
+
+        def hybrid(i):
+            group_sums(i)
+            ex = keep.tile([P, HALF], F32, name=f"ex{i}")
+            nc.scalar.activation(ex[:], shifted[i][:], ACT.Exp)
+            inv = keep.tile([P, P], F32, name=f"inv{i}")
+            nc.vector.reciprocal(inv[:], sums[i][:])
+            turned = psum.tile([P, P], F32, name=f"turned{i}", tag="logs", bufs=2)
+            nc.tensor.transpose(turned[:], inv[:], ident[:])
+            width = HALF // PIECES[i]
+            for j in range(PIECES[i]):
+                lo, hi = width * j, width * (j + 1)
+                prob = keep.tile([P, width], F32, name=f"prob{i}_{j}")
+                nc.vector.tensor_tensor(
+                    by_group(prob[:]), by_group(ex[:, lo:hi]), per_group(turned[:, lo // D : hi // D]), ALU.mult
+                )
                 finish(i, prob, lo, hi, f"{i}_{j}")
 
         def direct(i):
@@ -277,5 +337,7 @@ def tile_picked_ypuct_gum_p_kernel(tc, x_words, x_scales, w1, cnt, qv, offs, out
                 front(step)
                 if PATH[step] == "log":
                     group_sums(step)
+                elif PATH[step] == "hyb":
+                    hybrid(step)
                 else:
                     direct(step)

@@ -1,4 +1,3 @@
-import math
 from contextlib import ExitStack
 
 import concourse.mybir as mybir
@@ -19,30 +18,33 @@ ACT = mybir.ActivationFunctionType
 AXIS_X = mybir.AxisListType.X
 
 P = 128
-PASSES = K // 512
-HALF = 512
-GROUPS = HALF // D
+PACK = 4
+K_PASS = P * PACK
+PASSES = K // K_PASS
+QUADRANTS = P // 32
+SCALE_ROWS = 4
+WIDTH = 512
+NODES = WIDTH // D
+HALVES = S // WIDTH
+CHUNKS = [(block, half) for half in range(HALVES) for block in range(N // P)]
+LAST = len(CHUNKS) - 1
+TAIL_PIECES = 2
 
 GUESS_RATE, GUESS_BIAS, GUESS_SHIFT = 0.476, 1.057, -1.8014
-QUART_SCALE = math.sqrt(0.5)
-QUART_BIAS = -1.0 / (12.0 * QUART_SCALE**3)
-QUAD_SCALE = math.sqrt(1.0 / 3.0)
-QUAD_BIAS = -13.0 / (27.0 * QUAD_SCALE)
-LOG_SHIFT = GUESS_SHIFT - QUART_BIAS**4 - QUAD_BIAS**2
+FIX_SLOPE, FIX_RATE, FIX_BIAS = -0.5001885367254387, 2.000813667509747, 0.613735380081114
+LOG_SHIFT = -1.5510155588183339
 
-ENG_I = ["v", "v", "g", "g"]
-ENG_C = ["v", "v", "v", "v"]
-ENG_H = ["g", "v", "v", "v"]
-HOLD = (1, 1)
-ENG_M = ["","","",""]
-PATH = ["log", "log", "log", "dir"]
-LOADS = ["c0", "s0", "s1", "s2", "s3", "x0", "x1", "w0", "w1", "q0", "q1", "q2", "q3"]
-PIECES = [1, 1, 2, 2]
+
+def by_node(ap):
+    return ap.rearrange("p (v d) -> p v d", d=D)
+
+
+def per_node(ap):
+    return ap.unsqueeze(2).to_broadcast([P, ap.shape[1], D])
 
 
 def tile_picked_ypuct_gum_p_kernel(tc, x_words, x_scales, w1, cnt, qv, offs, out):
     nc = tc.nc
-    engines = {"v": nc.vector, "g": nc.gpsimd}
     with ExitStack() as ctx:
         keep = ctx.enter_context(tc.tile_pool(name="keep", bufs=1))
         psum = ctx.enter_context(tc.psum_pool(name="psum", bufs=1))
@@ -51,293 +53,219 @@ def tile_picked_ypuct_gum_p_kernel(tc, x_words, x_scales, w1, cnt, qv, offs, out
         nc.gpsimd.memset(planes[:].bitcast(I32), 0)
         offsets = keep.tile([P, S // 16], U16, name="offsets")
         nc.sync.dma_start(offsets[:], offs)
-        visits = keep.tile([P, 2, D], F32, name="visits")
-
-        chunks = [(mt, h) for h in range(S // HALF) for mt in range(N // P)]
-        q_tiles, words, w_raw = {}, {}, {}
-        for what in LOADS:
-            i = int(what[1])
-            if what[0] == "c":
-                nc.sync.dma_start(visits[:], cnt[0:1, :].rearrange("o (h p d) -> p (o h) d", h=2, d=D))
-            elif what[0] == "u":
-                g, mt = i // 2, i % 2
-                part = keep.tile([P, 4, P], F32, name=f"w_part{i}")
-                nc.sync.dma_start(
-                    part[:], w1[512 * g : 512 * (g + 1), P * mt : P * (mt + 1)].rearrange("(p t) n -> p t n", t=4)
-                )
-                w_raw[(g, mt)] = part[:]
-            elif what[0] == "s":
-                nc.sync.dma_start(
-                    planes[32 * i : 32 * i + 4 * PASSES, :].bitcast(I32),
-                    x_scales[:, 4 * i : 4 * i + 4, :].bitcast(I32),
-                )
-            elif what[0] == "q":
-                mt, h = chunks[i]
-                q = keep.tile([P, HALF], F32, name=f"q{i}")
-                nc.sync.dma_start(q[:], qv[P * mt : P * (mt + 1), HALF * h : HALF * (h + 1)])
-                q_tiles[i] = q
-            elif what[0] == "x":
-                table = keep.tile([P, T], I32, name=f"words{i}", align_bytes=64)
-                nc.sync.dma_start(table[:], x_words[i].rearrange("p n t -> p (n t)").bitcast(I32))
-                words[i] = table
-            else:
-                raw = keep.tile([P, 4, N], F32, name=f"w_raw{i}")
-                nc.sync.dma_start(raw[:], w1[512 * i : 512 * (i + 1), :].rearrange("(p t) n -> p t n", t=4))
-                for mt in range(2):
-                    w_raw[(i, mt)] = raw[:, :, P * mt : P * (mt + 1)]
+        visits = keep.tile([P, HALVES, D], F32, name="visits")
+        nc.sync.dma_start(visits[:], cnt[0:1, :].rearrange("o (h p d) -> p (o h) d", h=HALVES, d=D))
+        for quad in range(QUADRANTS):
+            nc.sync.dma_start(
+                planes[32 * quad : 32 * quad + SCALE_ROWS * PASSES, :].bitcast(I32),
+                x_scales[:, SCALE_ROWS * quad : SCALE_ROWS * (quad + 1), :].bitcast(I32),
+            )
+        words, w_raw, values = [], [], []
+        for g in range(PASSES):
+            table = keep.tile([P, T], I32, name=f"words{g}", align_bytes=64)
+            nc.sync.dma_start(table[:], x_words[g].rearrange("p n t -> p (n t)").bitcast(I32))
+            words.append(table)
+        for g in range(PASSES):
+            raw = keep.tile([P, PACK, N], F32, name=f"w_raw{g}")
+            nc.sync.dma_start(raw[:], w1[K_PASS * g : K_PASS * (g + 1), :].rearrange("(p t) n -> p t n", t=PACK))
+            w_raw.append(raw)
+        for i, (block, half) in enumerate(CHUNKS):
+            value = keep.tile([P, WIDTH], F32, name=f"values{i}")
+            nc.sync.dma_start(value[:], qv[P * block : P * (block + 1), WIDTH * half : WIDTH * (half + 1)])
+            values.append(value)
 
         ident = keep.tile([P, P], F32, name="ident")
         make_identity(nc, ident[:])
 
-        most = keep.tile([P, 2], F32, name="most")
-        nc.vector.tensor_reduce(most[:], visits[:], AXIS_X, ALU.max)
-        total = keep.tile([P, 2], F32, name="total")
-        padded = keep.tile([P, 2, D], F32, name="padded")
-        for h in range(2):
-            nc.scalar.activation(
-                padded[:, h, :], visits[:, h, :], ACT.Identity, bias=1.0 / D, accum_out=total[:, h : h + 1]
-            )
-        inv_total = keep.tile([P, 2], F32, name="inv_total")
-        nc.vector.reciprocal(inv_total[:], total[:])
-        share_col = keep.tile([P, 2, D], F32, name="share_col")
-        for h in range(2):
-            nc.scalar.activation(share_col[:, h, :], visits[:, h, :], ACT.Copy, scale=inv_total[:, h : h + 1])
+        def spread(dst, column):
+            nc.tensor.transpose(dst, column.to_broadcast([P, P]), ident[:])
 
-        weight = keep.tile([P, S], F32, name="weight")
-        weight_col = keep.tile([P, 2], F32, name="weight_col")
-        nc.scalar.activation(weight_col[:], most[:], ACT.Identity, bias=0.03 * 50.0, scale=0.03)
-        weight_ps = psum.tile([P, 2 * P], F32, name="weight_ps")
-        for h in range(2):
-            nc.tensor.transpose(
-                weight_ps[:, P * h : P * (h + 1)], weight_col[:, h : h + 1].to_broadcast([P, P]), ident[:]
+        most = keep.tile([P, HALVES], F32, name="most")
+        nc.vector.tensor_reduce(most[:], visits[:], AXIS_X, ALU.max)
+        count_sum = keep.tile([P, HALVES], F32, name="count_sum")
+        padded = keep.tile([P, HALVES, D], F32, name="padded")
+        for half in range(HALVES):
+            nc.scalar.activation(
+                padded[:, half, :], visits[:, half, :], ACT.Identity, bias=1.0 / D,
+                accum_out=count_sum[:, half : half + 1],
             )
-        for h in range(2):
-            if any(ENG_I[i] == "g" and chunks[i][1] == h for i in range(len(chunks))):
-                nc.scalar.copy(
-                    weight[:, HALF * h : HALF * (h + 1)].rearrange("p (v d) -> p v d", d=D),
-                    weight_ps[:, P * h : P * (h + 1)].unsqueeze(2).to_broadcast([P, P, D]),
-                )
-        share = keep.tile([P, S], F32, name="share")
-        share_ps = {}
-        for h in range(2):
-            if h == 0:
-                spread = psum.tile([P, HALF], F32, name="spread_s0", tag="wide", bufs=2)
-            else:
-                spread = psum.tile([P, HALF], F32, name="spread_s1")
-            share_ps[h] = spread
-            for d in range(D):
-                nc.tensor.transpose(
-                    spread[:, P * d : P * (d + 1)], share_col[:, h, d : d + 1].to_broadcast([P, P]), ident[:]
-                )
-            if h == 0 or any(ENG_H[i] == "g" and chunks[i][1] == h for i in range(len(chunks))):
-              nc.scalar.copy(
-                share[:, HALF * h : HALF * (h + 1)].rearrange("p (v d) -> p v d", d=D),
-                spread[:].rearrange("p (d v) -> p v d", d=D),
+        inv_count_sum = keep.tile([P, HALVES], F32, name="inv_count_sum")
+        nc.vector.reciprocal(inv_count_sum[:], count_sum[:])
+        share_col = keep.tile([P, HALVES, D], F32, name="share_col")
+        for half in range(HALVES):
+            nc.scalar.activation(
+                share_col[:, half, :], visits[:, half, :], ACT.Copy, scale=inv_count_sum[:, half : half + 1]
             )
+        factor_col = keep.tile([P, HALVES], F32, name="factor_col")
+        nc.scalar.activation(factor_col[:], most[:], ACT.Identity, bias=0.03 * 50.0, scale=0.03)
+
+        factor_psum = psum.tile([P, HALVES, NODES], F32, name="factor_psum")
+        for half in range(HALVES):
+            spread(factor_psum[:, half, :], factor_col[:, half : half + 1])
+        factor_sbuf = keep.tile([P, WIDTH], F32, name="factor_sbuf")
+        nc.scalar.copy(by_node(factor_sbuf[:]), per_node(factor_psum[:, 1, :]))
+        share_staged = psum.tile([P, D, NODES], F32, name="share_staged", tag="product", bufs=2)
+        for d in range(D):
+            spread(share_staged[:, d, :], share_col[:, 0, d : d + 1])
+        share_sbuf = keep.tile([P, WIDTH], F32, name="share_sbuf")
+        nc.scalar.copy(by_node(share_sbuf[:]), share_staged[:].rearrange("p d v -> p v d"))
+        share_psum = psum.tile([P, D, NODES], F32, name="share_psum")
+        for d in range(D):
+            spread(share_psum[:, d, :], share_col[:, 1, d : d + 1])
 
         picked_planes = keep.tile([P, S], U8, name="picked_planes", align_bytes=64)
         nc.vector.tensor_copy(picked_planes[:], planes[:].indirect(offsets[:]))
-        picked0 = keep.tile([P, S], U32, name="picked0", align_bytes=64)
-        nc.vector.tensor_copy(picked0[:], words[0][:].bitcast(U32).indirect(offsets[:]))
-        picked = {(0, h): picked0[:, HALF * h : HALF * (h + 1)] for h in range(2)}
+        picked_first = keep.tile([P, S], U32, name="picked_first", align_bytes=64)
+        nc.vector.tensor_copy(picked_first[:], words[0][:].bitcast(U32).indirect(offsets[:]))
+        picked = {(0, half): picked_first[:, WIDTH * half : WIDTH * (half + 1)] for half in range(HALVES)}
 
-        def gather_last(h):
-            tile = keep.tile([P, HALF], U32, name=f"picked1_{h}", align_bytes=64)
-            cols = HALF // 16
+        def gather_last_pass(half):
+            tile = keep.tile([P, WIDTH], U32, name=f"picked_last{half}", align_bytes=64)
+            columns = WIDTH // 16
             nc.vector.tensor_copy(
-                tile[:], words[1][:].bitcast(U32).indirect(offsets[:, cols * h : cols * (h + 1)])
+                tile[:], words[1][:].bitcast(U32).indirect(offsets[:, columns * half : columns * (half + 1)])
             )
-            picked[(1, h)] = tile[:]
+            picked[(1, half)] = tile[:]
 
         w_codes, w_scales = {}, {}
 
-        def quantise(g, mt):
-            grouped = keep.tile(
-                [P, P, 4], BF16, name=f"w_bf{g}{mt}", tag="handover" if (g, mt) == HOLD else f"w_bf{g}{mt}", align_bytes=64
-            )
+        def quantise(g, block, tag):
+            grouped = keep.tile([P, P, PACK], BF16, name=f"grouped{g}{block}", tag=tag, align_bytes=64)
             nc.scalar.copy(
                 grouped[:].rearrange("p (c i) t -> p c t i", i=4),
-                w_raw[(g, mt)].rearrange("p t (c i) -> p c t i", i=4),
+                w_raw[g][:, :, P * block : P * (block + 1)].rearrange("p t (c i) -> p c t i", i=4),
             )
-            codes = keep.tile([P, P], U32, name=f"w_codes{g}{mt}", align_bytes=64)
-            scales = keep.tile([P, P], U8, name=f"w_scales{g}{mt}", align_bytes=64)
+            codes = keep.tile([P, P], U32, name=f"w_codes{g}{block}", align_bytes=64)
+            scales = keep.tile([P, P], U8, name=f"w_scales{g}{block}", align_bytes=64)
             nc.vector.quantize_mx(
                 out=codes[:].bitcast(FP8X4), scales=scales[:], in_=grouped[:].rearrange("p m t -> p (m t)")
             )
-            w_codes[(g, mt)], w_scales[(g, mt)] = codes, scales
+            w_codes[(g, block)], w_scales[(g, block)] = codes, scales
 
-        gather_last(0)
-        quantise(0, 0)
-        quantise(0, 1)
-        quantise(1, 0)
-        quantise(1, 1)
-        gather_last(1)
+        gather_last_pass(0)
+        quantise(0, 0, "grouped00")
+        quantise(0, 1, "grouped01")
+        quantise(1, 0, "grouped10")
+        quantise(1, 1, "handover")
+        gather_last_pass(1)
 
-        def by_group(ap):
-            return ap.rearrange("p (v d) -> p v d", d=D)
-
-        def per_group(ap):
-            return ap.unsqueeze(2).to_broadcast([P, ap.shape[1], D])
-
-        weighted, shifted, sums, logs, plain = {}, {}, {}, {}, {}
-        late = keep.tile([P, HALF * max(1, len([e for e in ENG_I if e == "g"]))], F32, name="late", tag="handover", align_bytes=64)
-
-        def weigh(i):
-            mt, h = chunks[i]
-            if ENG_I[i] == "g":
-                slot = len([e for e in ENG_I[:i] if e == "g"])
-                tile = late[:, HALF * slot : HALF * (slot + 1)]
-                nc.gpsimd.tensor_tensor(tile, q_tiles[i][:], weight[:, HALF * h : HALF * (h + 1)], ALU.mult)
-            else:
-                whole = keep.tile([P, HALF], F32, name=f"weighted{i}")
-                tile = whole[:]
+        weighted_late = keep.tile([P, N // P, WIDTH], F32, name="weighted_late", tag="handover", align_bytes=64)
+        weighted = []
+        for i, (block, half) in enumerate(CHUNKS):
+            if half == 0:
+                early = keep.tile([P, WIDTH], F32, name=f"weighted{i}")
                 nc.vector.tensor_tensor(
-                    by_group(tile), by_group(q_tiles[i][:]),
-                    per_group(weight_ps[:, GROUPS * h : GROUPS * (h + 1)]), ALU.mult,
+                    by_node(early[:]), by_node(values[i][:]), per_node(factor_psum[:, 0, :]), ALU.mult
                 )
-            weighted[i] = tile
+                weighted.append(early[:])
+            else:
+                nc.gpsimd.tensor_tensor(weighted_late[:, block, :], values[i][:], factor_sbuf[:], ALU.mult)
+                weighted.append(weighted_late[:, block, :])
 
-        def front(i):
-            mt, h = chunks[i]
-            cols = slice(HALF * h, HALF * (h + 1))
-            y = psum.tile([P, HALF], F32, name=f"y{i}", tag="wide", bufs=2)
-            order = list(range(PASSES)) if mt == 0 else list(reversed(range(PASSES)))
+        def product(i):
+            block, half = CHUNKS[i]
+            y = psum.tile([P, WIDTH], F32, name=f"y{i}", tag="product", bufs=2)
+            order = list(range(PASSES)) if block == 0 else list(reversed(range(PASSES)))
             for g in order:
                 nc.tensor.matmul_mx(
                     out=y[:],
-                    lhsT=w_codes[(g, mt)][:].bitcast(FP8X4),
-                    lhsT_scale=w_scales[(g, mt)][:],
-                    rhs=picked[(g, h)].bitcast(FP8X4),
-                    rhs_scale=picked_planes[4 * g : P, cols],
+                    lhsT=w_codes[(g, block)][:].bitcast(FP8X4),
+                    lhsT_scale=w_scales[(g, block)][:],
+                    rhs=picked[(g, half)].bitcast(FP8X4),
+                    rhs_scale=picked_planes[SCALE_ROWS * g : P, WIDTH * half : WIDTH * (half + 1)],
                     start=(g == order[0]),
                     stop=(g == order[-1]),
                 )
-            z = keep.tile([P, HALF], F32, name=f"z{i}")
-            nc.vector.tensor_tensor(z[:], y[:], weighted[i], ALU.add)
-            top = keep.tile([P, GROUPS], F32, name=f"top{i}")
-            nc.vector.tensor_reduce(top[:], by_group(z[:]), AXIS_X, ALU.max)
-            low = keep.tile([P, HALF], F32, name=f"low{i}")
-            engines[ENG_C[i]].tensor_tensor(by_group(low[:]), by_group(z[:]), per_group(top[:]), ALU.subtract)
-            shifted[i] = low
+            return y
 
-        def group_sums(i):
-            dealt = keep.tile([P, D, GROUPS], F32, name=f"dealt{i}")
-            nc.scalar.activation(dealt[:].rearrange("p d v -> p v d"), by_group(shifted[i][:]), ACT.Exp)
-            ts = psum.tile([P, P], F32, name=f"ts{i}", tag="sums", bufs=2)
-            for d in range(D):
-                nc.tensor.matmul(
-                    ts[:], dealt[:, d, :], ident[:], start=(d == 0), stop=(d == D - 1), is_transpose=True
-                )
-            sums[i] = ts
-
-        def middle(i):
-            ts = sums[i]
-            guess = keep.tile([P, P], F32, name=f"guess{i}")
-            nc.scalar.activation(guess[:], ts[:], ACT.Exp, bias=GUESS_BIAS, scale=-GUESS_RATE)
-            inverse = keep.tile([P, P], F32, name=f"inverse{i}")
-            nc.scalar.activation(inverse[:], guess[:], ACT.Exp, bias=GUESS_SHIFT)
-            near_one = keep.tile([P, P], F32, name=f"near_one{i}")
-            nc.vector.tensor_tensor(near_one[:], ts[:], inverse[:], ALU.mult)
-            root = keep.tile([P, P], F32, name=f"root{i}")
-            nc.scalar.activation(root[:], near_one[:], ACT.Square, bias=QUART_BIAS - QUART_SCALE, scale=QUART_SCALE)
-            quad = keep.tile([P, P], F32, name=f"quad{i}")
-            nc.scalar.activation(quad[:], near_one[:], ACT.Square, bias=QUAD_BIAS - QUAD_SCALE, scale=QUAD_SCALE)
-            quart = keep.tile([P, P], F32, name=f"quart{i}")
-            nc.scalar.activation(quart[:], root[:], ACT.Square)
-            neg_log = psum.tile([P, P], F32, name=f"neg_log{i}", tag="logs", bufs=2)
-            terms = (guess, quad, quart)
+        def add_turned(dst, terms):
             for j, term in enumerate(terms):
                 nc.tensor.matmul(
-                    neg_log[:], term[:], ident[:], start=(j == 0), stop=(j == len(terms) - 1), is_transpose=True
+                    dst, term, ident[:], start=(j == 0), stop=(j == len(terms) - 1), is_transpose=True
                 )
-            logs[i] = neg_log
-            if ENG_M[i] != "":
-                ex = keep.tile([P, HALF], F32, name=f"ex{i}")
-                nc.scalar.activation(ex[:], shifted[i][:], ACT.Exp)
-                plain[i] = ex
 
-        def finish(i, prob, lo, hi, tag):
-            mt, h = chunks[i]
-            result = keep.tile([P, hi - lo], F32, name=f"result{tag}")
-            cols = slice(HALF * h + lo, HALF * h + hi)
-            if ENG_H[i] == "g" or h == 0:
-                engines[ENG_H[i]].tensor_tensor(result[:], prob[:], share[:, cols], ALU.subtract)
+        shifted, totals, neg_logs = {}, {}, {}
+
+        def shift(i):
+            y = product(i)
+            z = keep.tile([P, WIDTH], F32, name=f"z{i}")
+            nc.vector.tensor_tensor(z[:], y[:], weighted[i], ALU.add)
+            top = keep.tile([P, NODES], F32, name=f"top{i}")
+            nc.vector.tensor_reduce(top[:], by_node(z[:]), AXIS_X, ALU.max)
+            low = keep.tile([P, WIDTH], F32, name=f"shifted{i}")
+            nc.vector.tensor_tensor(by_node(low[:]), by_node(z[:]), per_node(top[:]), ALU.subtract)
+            shifted[i] = low
+
+        def sum_children(i):
+            dealt = keep.tile([P, D, NODES], F32, name=f"dealt{i}")
+            nc.scalar.activation(dealt[:].rearrange("p d v -> p v d"), by_node(shifted[i][:]), ACT.Exp)
+            total = psum.tile([NODES, P], F32, name=f"total{i}", tag="total", bufs=2)
+            add_turned(total[:], [dealt[:, d, :] for d in range(D)])
+            totals[i] = total
+
+        def negative_log(i):
+            guess = keep.tile([NODES, P], F32, name=f"guess{i}")
+            nc.scalar.activation(guess[:], totals[i][:], ACT.Exp, bias=GUESS_BIAS, scale=-GUESS_RATE)
+            inverse = keep.tile([NODES, P], F32, name=f"inverse{i}")
+            nc.scalar.activation(inverse[:], guess[:], ACT.Exp, bias=GUESS_SHIFT)
+            linear = keep.tile([NODES, P], F32, name=f"linear{i}")
+            nc.vector.scalar_tensor_tensor(linear[:], totals[i][:], FIX_SLOPE, inverse[:], ALU.mult, ALU.mult)
+            curved = keep.tile([NODES, P], F32, name=f"curved{i}")
+            nc.scalar.activation(curved[:], linear[:], ACT.Exp, bias=FIX_BIAS, scale=-FIX_RATE / FIX_SLOPE)
+            neg_log = psum.tile([P, NODES], F32, name=f"neg_log{i}", tag="neg_log", bufs=2)
+            add_turned(neg_log[:], [guess[:], linear[:], curved[:]])
+            neg_logs[i] = neg_log
+
+        def pieces(i):
+            span = NODES if CHUNKS[i][1] == 0 else NODES // TAIL_PIECES
+            return [(slice(v, v + span), slice(D * v, D * (v + span))) for v in range(0, NODES, span)]
+
+        def take_off_shares(i, prob, nodes, entries):
+            block, half = CHUNKS[i]
+            result = keep.tile(list(prob.shape), F32, name=f"result{i}_{nodes.start}")
+            if half == 0:
+                engine = nc.gpsimd if i == 0 else nc.vector
+                engine.tensor_tensor(result[:], prob[:], share_sbuf[:, entries], ALU.subtract)
             else:
                 nc.vector.tensor_tensor(
-                    by_group(result[:]), by_group(prob[:]),
-                    share_ps[h][:].rearrange("p (d v) -> p v d", d=D)[:, lo // D : hi // D, :], ALU.subtract,
+                    by_node(result[:]), by_node(prob[:]),
+                    share_psum[:].rearrange("p d v -> p v d")[:, nodes, :], ALU.subtract,
                 )
-            nc.sync.dma_start(out[P * mt : P * (mt + 1), cols], result[:])
+            columns = slice(WIDTH * half + entries.start, WIDTH * half + entries.stop)
+            nc.sync.dma_start(out[P * block : P * (block + 1), columns], result[:])
 
-        def back_mul(i):
-            inv = keep.tile([P, P], F32, name=f"inv{i}")
-            nc.scalar.activation(inv[:], logs[i][:], ACT.Exp, bias=LOG_SHIFT)
-            width = HALF // PIECES[i]
-            for j in range(PIECES[i]):
-                lo, hi = width * j, width * (j + 1)
-                prob = keep.tile([P, width], F32, name=f"prob{i}_{j}")
-                engines[ENG_M[i]].tensor_tensor(
-                    by_group(prob[:]), by_group(plain[i][:, lo:hi]), per_group(inv[:, lo // D : hi // D]), ALU.mult
-                )
-                finish(i, prob, lo, hi, f"{i}_{j}")
-
-        def back(i):
-            if ENG_M[i] != "":
-                return back_mul(i)
-            width = HALF // PIECES[i]
-            for j in range(PIECES[i]):
-                lo, hi = width * j, width * (j + 1)
-                logp = keep.tile([P, width], F32, name=f"logp{i}_{j}")
+        def finish_by_log(i):
+            for nodes, entries in pieces(i):
+                width = entries.stop - entries.start
+                log_prob = keep.tile([P, width], F32, name=f"log_prob{i}_{nodes.start}")
                 nc.vector.tensor_tensor(
-                    by_group(logp[:]), by_group(shifted[i][:, lo:hi]), per_group(logs[i][:, lo // D : hi // D]), ALU.add
+                    by_node(log_prob[:]), by_node(shifted[i][:, entries]), per_node(neg_logs[i][:, nodes]), ALU.add
                 )
-                prob = keep.tile([P, width], F32, name=f"prob{i}_{j}")
-                nc.scalar.activation(prob[:], logp[:], ACT.Exp, bias=LOG_SHIFT)
-                finish(i, prob, lo, hi, f"{i}_{j}")
+                prob = keep.tile([P, width], F32, name=f"prob{i}_{nodes.start}")
+                nc.scalar.activation(prob[:], log_prob[:], ACT.Exp, bias=LOG_SHIFT)
+                take_off_shares(i, prob, nodes, entries)
 
-        def hybrid(i):
-            group_sums(i)
-            ex = keep.tile([P, HALF], F32, name=f"ex{i}")
-            nc.scalar.activation(ex[:], shifted[i][:], ACT.Exp)
-            inv = keep.tile([P, P], F32, name=f"inv{i}")
-            nc.vector.reciprocal(inv[:], sums[i][:])
-            turned = psum.tile([P, P], F32, name=f"turned{i}", tag="logs", bufs=2)
-            nc.tensor.transpose(turned[:], inv[:], ident[:])
-            width = HALF // PIECES[i]
-            for j in range(PIECES[i]):
-                lo, hi = width * j, width * (j + 1)
-                prob = keep.tile([P, width], F32, name=f"prob{i}_{j}")
-                nc.vector.tensor_tensor(
-                    by_group(prob[:]), by_group(ex[:, lo:hi]), per_group(turned[:, lo // D : hi // D]), ALU.mult
-                )
-                finish(i, prob, lo, hi, f"{i}_{j}")
+        def finish_by_reciprocal(i):
+            for nodes, entries in pieces(i):
+                width = entries.stop - entries.start
+                ex = keep.tile([P, width], F32, name=f"ex{i}_{nodes.start}")
+                nc.scalar.activation(ex[:], shifted[i][:, entries], ACT.Exp)
+                ex_sum = keep.tile([P, width // D], F32, name=f"ex_sum{i}_{nodes.start}")
+                nc.vector.tensor_reduce(ex_sum[:], by_node(ex[:]), AXIS_X, ALU.add)
+                inv_sum = keep.tile([P, width // D], F32, name=f"inv_sum{i}_{nodes.start}")
+                nc.vector.reciprocal(inv_sum[:], ex_sum[:])
+                prob = keep.tile([P, width], F32, name=f"prob{i}_{nodes.start}")
+                nc.vector.tensor_tensor(by_node(prob[:]), by_node(ex[:]), per_node(inv_sum[:]), ALU.mult)
+                take_off_shares(i, prob, nodes, entries)
 
-        def direct(i):
-            width = HALF // PIECES[i]
-            for j in range(PIECES[i]):
-                lo, hi = width * j, width * (j + 1)
-                ex = keep.tile([P, width], F32, name=f"ex{i}_{j}")
-                nc.scalar.activation(ex[:], shifted[i][:, lo:hi], ACT.Exp)
-                ts = keep.tile([P, width // D], F32, name=f"sum{i}_{j}")
-                nc.vector.tensor_reduce(ts[:], by_group(ex[:]), AXIS_X, ALU.add)
-                inv = keep.tile([P, width // D], F32, name=f"inv{i}_{j}")
-                nc.vector.reciprocal(inv[:], ts[:])
-                prob = keep.tile([P, width], F32, name=f"prob{i}_{j}")
-                nc.vector.tensor_tensor(by_group(prob[:]), by_group(ex[:]), per_group(inv[:]), ALU.mult)
-                finish(i, prob, lo, hi, f"{i}_{j}")
-
-        for i in range(len(chunks)):
-            weigh(i)
-        for step in range(len(chunks) + 2):
-            if 0 <= step - 2 < len(chunks) and PATH[step - 2] == "log":
-                back(step - 2)
-            if 0 <= step - 1 < len(chunks) and PATH[step - 1] == "log":
-                middle(step - 1)
-            if step < len(chunks):
-                front(step)
-                if PATH[step] == "log":
-                    group_sums(step)
-                elif PATH[step] == "hyb":
-                    hybrid(step)
-                else:
-                    direct(step)
+        for step in range(LAST + 2):
+            if 0 <= step - 2 < LAST:
+                finish_by_log(step - 2)
+            if 0 <= step - 1 < LAST:
+                negative_log(step - 1)
+            if step < LAST:
+                shift(step)
+                sum_children(step)
+            elif step == LAST:
+                shift(step)
+                finish_by_reciprocal(step)

from contextlib import ExitStack

import concourse.mybir as mybir
from concourse.masks import make_identity

K, T, S, D, N = 1024, 2048, 1024, 4, 256
FLOPS = 2 * K * S * N

F32 = mybir.dt.float32
BF16 = mybir.dt.bfloat16
I32 = mybir.dt.int32
U32 = mybir.dt.uint32
U16 = mybir.dt.uint16
U8 = mybir.dt.uint8
FP8X4 = mybir.dt.float8_e4m3fn_x4
ALU = mybir.AluOpType
ACT = mybir.ActivationFunctionType
AXIS_X = mybir.AxisListType.X

P = 128
PACK = 4
K_PASS = P * PACK
PASSES = K // K_PASS
QUADRANTS = P // 32
SCALE_ROWS = 4
WIDTH = 512
NODES = WIDTH // D
HALVES = S // WIDTH
CHUNKS = [(block, half) for half in range(HALVES) for block in range(N // P)]
LAST = len(CHUNKS) - 1
TAIL_PIECES = 2

GUESS_RATE, GUESS_BIAS, GUESS_SHIFT = 0.476, 1.057, -1.8014
FIX_SLOPE, FIX_RATE, FIX_BIAS = -0.5001885367254387, 2.000813667509747, 0.613735380081114
LOG_SHIFT = -1.5510155588183339


def by_node(ap):
    return ap.rearrange("p (v d) -> p v d", d=D)


def per_node(ap):
    return ap.unsqueeze(2).to_broadcast([P, ap.shape[1], D])


def tile_picked_ypuct_gum_p_kernel(tc, x_words, x_scales, w1, cnt, qv, offs, out):
    nc = tc.nc
    with ExitStack() as ctx:
        keep = ctx.enter_context(tc.tile_pool(name="keep", bufs=1))
        psum = ctx.enter_context(tc.psum_pool(name="psum", bufs=1))

        planes = keep.tile([P, T], U8, name="planes", align_bytes=64)
        nc.gpsimd.memset(planes[:].bitcast(I32), 0)
        offsets = keep.tile([P, S // 16], U16, name="offsets")
        nc.sync.dma_start(offsets[:], offs)
        visits = keep.tile([P, HALVES, D], F32, name="visits")
        nc.sync.dma_start(visits[:], cnt[0:1, :].rearrange("o (h p d) -> p (o h) d", h=HALVES, d=D))
        for quad in range(QUADRANTS):
            nc.sync.dma_start(
                planes[32 * quad : 32 * quad + SCALE_ROWS * PASSES, :].bitcast(I32),
                x_scales[:, SCALE_ROWS * quad : SCALE_ROWS * (quad + 1), :].bitcast(I32),
            )
        words, w_raw, values = [], [], []
        for g in range(PASSES):
            table = keep.tile([P, T], I32, name=f"words{g}", align_bytes=64)
            nc.sync.dma_start(table[:], x_words[g].rearrange("p n t -> p (n t)").bitcast(I32))
            words.append(table)
        for g in range(PASSES):
            raw = keep.tile([P, PACK, N], F32, name=f"w_raw{g}")
            nc.sync.dma_start(raw[:], w1[K_PASS * g : K_PASS * (g + 1), :].rearrange("(p t) n -> p t n", t=PACK))
            w_raw.append(raw)
        for i, (block, half) in enumerate(CHUNKS):
            value = keep.tile([P, WIDTH], F32, name=f"values{i}")
            nc.sync.dma_start(value[:], qv[P * block : P * (block + 1), WIDTH * half : WIDTH * (half + 1)])
            values.append(value)

        ident = keep.tile([P, P], F32, name="ident")
        make_identity(nc, ident[:])

        def spread(dst, column):
            nc.tensor.transpose(dst, column.to_broadcast([P, P]), ident[:])

        most = keep.tile([P, HALVES], F32, name="most")
        nc.vector.tensor_reduce(most[:], visits[:], AXIS_X, ALU.max)
        count_sum = keep.tile([P, HALVES], F32, name="count_sum")
        padded = keep.tile([P, HALVES, D], F32, name="padded")
        for half in range(HALVES):
            nc.scalar.activation(
                padded[:, half, :], visits[:, half, :], ACT.Identity, bias=1.0 / D,
                accum_out=count_sum[:, half : half + 1],
            )
        inv_count_sum = keep.tile([P, HALVES], F32, name="inv_count_sum")
        nc.vector.reciprocal(inv_count_sum[:], count_sum[:])
        share_col = keep.tile([P, HALVES, D], F32, name="share_col")
        for half in range(HALVES):
            nc.scalar.activation(
                share_col[:, half, :], visits[:, half, :], ACT.Copy, scale=inv_count_sum[:, half : half + 1]
            )
        factor_col = keep.tile([P, HALVES], F32, name="factor_col")
        nc.scalar.activation(factor_col[:], most[:], ACT.Identity, bias=0.03 * 50.0, scale=0.03)

        factor_psum = psum.tile([P, HALVES, NODES], F32, name="factor_psum")
        for half in range(HALVES):
            spread(factor_psum[:, half, :], factor_col[:, half : half + 1])
        factor_sbuf = keep.tile([P, WIDTH], F32, name="factor_sbuf")
        nc.scalar.copy(by_node(factor_sbuf[:]), per_node(factor_psum[:, 1, :]))
        share_staged = psum.tile([P, D, NODES], F32, name="share_staged", tag="product", bufs=2)
        for d in range(D):
            spread(share_staged[:, d, :], share_col[:, 0, d : d + 1])
        share_sbuf = keep.tile([P, WIDTH], F32, name="share_sbuf")
        nc.scalar.copy(by_node(share_sbuf[:]), share_staged[:].rearrange("p d v -> p v d"))
        share_psum = psum.tile([P, D, NODES], F32, name="share_psum")
        for d in range(D):
            spread(share_psum[:, d, :], share_col[:, 1, d : d + 1])

        picked_planes = keep.tile([P, S], U8, name="picked_planes", align_bytes=64)
        nc.vector.tensor_copy(picked_planes[:], planes[:].indirect(offsets[:]))
        picked_first = keep.tile([P, S], U32, name="picked_first", align_bytes=64)
        nc.vector.tensor_copy(picked_first[:], words[0][:].bitcast(U32).indirect(offsets[:]))
        picked = {(0, half): picked_first[:, WIDTH * half : WIDTH * (half + 1)] for half in range(HALVES)}

        def gather_last_pass(half):
            tile = keep.tile([P, WIDTH], U32, name=f"picked_last{half}", align_bytes=64)
            columns = WIDTH // 16
            nc.vector.tensor_copy(
                tile[:], words[1][:].bitcast(U32).indirect(offsets[:, columns * half : columns * (half + 1)])
            )
            picked[(1, half)] = tile[:]

        w_codes, w_scales = {}, {}

        def quantise(g, block, tag):
            grouped = keep.tile([P, P, PACK], BF16, name=f"grouped{g}{block}", tag=tag, align_bytes=64)
            nc.scalar.copy(
                grouped[:].rearrange("p (c i) t -> p c t i", i=4),
                w_raw[g][:, :, P * block : P * (block + 1)].rearrange("p t (c i) -> p c t i", i=4),
            )
            codes = keep.tile([P, P], U32, name=f"w_codes{g}{block}", align_bytes=64)
            scales = keep.tile([P, P], U8, name=f"w_scales{g}{block}", align_bytes=64)
            nc.vector.quantize_mx(
                out=codes[:].bitcast(FP8X4), scales=scales[:], in_=grouped[:].rearrange("p m t -> p (m t)")
            )
            w_codes[(g, block)], w_scales[(g, block)] = codes, scales

        gather_last_pass(0)
        quantise(0, 0, "grouped00")
        quantise(0, 1, "grouped01")
        quantise(1, 0, "grouped10")
        quantise(1, 1, "handover")
        gather_last_pass(1)

        weighted_late = keep.tile([P, N // P, WIDTH], F32, name="weighted_late", tag="handover", align_bytes=64)
        weighted = []
        for i, (block, half) in enumerate(CHUNKS):
            if half == 0:
                early = keep.tile([P, WIDTH], F32, name=f"weighted{i}")
                nc.vector.tensor_tensor(
                    by_node(early[:]), by_node(values[i][:]), per_node(factor_psum[:, 0, :]), ALU.mult
                )
                weighted.append(early[:])
            else:
                nc.gpsimd.tensor_tensor(weighted_late[:, block, :], values[i][:], factor_sbuf[:], ALU.mult)
                weighted.append(weighted_late[:, block, :])

        def product(i):
            block, half = CHUNKS[i]
            y = psum.tile([P, WIDTH], F32, name=f"y{i}", tag="product", bufs=2)
            order = list(range(PASSES)) if block == 0 else list(reversed(range(PASSES)))
            for g in order:
                nc.tensor.matmul_mx(
                    out=y[:],
                    lhsT=w_codes[(g, block)][:].bitcast(FP8X4),
                    lhsT_scale=w_scales[(g, block)][:],
                    rhs=picked[(g, half)].bitcast(FP8X4),
                    rhs_scale=picked_planes[SCALE_ROWS * g : P, WIDTH * half : WIDTH * (half + 1)],
                    start=(g == order[0]),
                    stop=(g == order[-1]),
                )
            return y

        def add_turned(dst, terms):
            for j, term in enumerate(terms):
                nc.tensor.matmul(
                    dst, term, ident[:], start=(j == 0), stop=(j == len(terms) - 1), is_transpose=True
                )

        shifted, totals, neg_logs = {}, {}, {}

        def shift(i):
            y = product(i)
            z = keep.tile([P, WIDTH], F32, name=f"z{i}")
            nc.vector.tensor_tensor(z[:], y[:], weighted[i], ALU.add)
            top = keep.tile([P, NODES], F32, name=f"top{i}")
            nc.vector.tensor_reduce(top[:], by_node(z[:]), AXIS_X, ALU.max)
            low = keep.tile([P, WIDTH], F32, name=f"shifted{i}")
            nc.vector.tensor_tensor(by_node(low[:]), by_node(z[:]), per_node(top[:]), ALU.subtract)
            shifted[i] = low

        def sum_children(i):
            dealt = keep.tile([P, D, NODES], F32, name=f"dealt{i}")
            nc.scalar.activation(dealt[:].rearrange("p d v -> p v d"), by_node(shifted[i][:]), ACT.Exp)
            total = psum.tile([NODES, P], F32, name=f"total{i}", tag="total", bufs=2)
            add_turned(total[:], [dealt[:, d, :] for d in range(D)])
            totals[i] = total

        def negative_log(i):
            guess = keep.tile([NODES, P], F32, name=f"guess{i}")
            nc.scalar.activation(guess[:], totals[i][:], ACT.Exp, bias=GUESS_BIAS, scale=-GUESS_RATE)
            inverse = keep.tile([NODES, P], F32, name=f"inverse{i}")
            nc.scalar.activation(inverse[:], guess[:], ACT.Exp, bias=GUESS_SHIFT)
            linear = keep.tile([NODES, P], F32, name=f"linear{i}")
            nc.vector.scalar_tensor_tensor(linear[:], totals[i][:], FIX_SLOPE, inverse[:], ALU.mult, ALU.mult)
            curved = keep.tile([NODES, P], F32, name=f"curved{i}")
            nc.scalar.activation(curved[:], linear[:], ACT.Exp, bias=FIX_BIAS, scale=-FIX_RATE / FIX_SLOPE)
            neg_log = psum.tile([P, NODES], F32, name=f"neg_log{i}", tag="neg_log", bufs=2)
            add_turned(neg_log[:], [guess[:], linear[:], curved[:]])
            neg_logs[i] = neg_log

        def pieces(i):
            span = NODES if CHUNKS[i][1] == 0 else NODES // TAIL_PIECES
            return [(slice(v, v + span), slice(D * v, D * (v + span))) for v in range(0, NODES, span)]

        def take_off_shares(i, prob, nodes, entries):
            block, half = CHUNKS[i]
            result = keep.tile(list(prob.shape), F32, name=f"result{i}_{nodes.start}")
            if half == 0:
                engine = nc.gpsimd if i == 0 else nc.vector
                engine.tensor_tensor(result[:], prob[:], share_sbuf[:, entries], ALU.subtract)
            else:
                nc.vector.tensor_tensor(
                    by_node(result[:]), by_node(prob[:]),
                    share_psum[:].rearrange("p d v -> p v d")[:, nodes, :], ALU.subtract,
                )
            columns = slice(WIDTH * half + entries.start, WIDTH * half + entries.stop)
            nc.sync.dma_start(out[P * block : P * (block + 1), columns], result[:])

        def finish_by_log(i):
            for nodes, entries in pieces(i):
                width = entries.stop - entries.start
                log_prob = keep.tile([P, width], F32, name=f"log_prob{i}_{nodes.start}")
                nc.vector.tensor_tensor(
                    by_node(log_prob[:]), by_node(shifted[i][:, entries]), per_node(neg_logs[i][:, nodes]), ALU.add
                )
                prob = keep.tile([P, width], F32, name=f"prob{i}_{nodes.start}")
                nc.scalar.activation(prob[:], log_prob[:], ACT.Exp, bias=LOG_SHIFT)
                take_off_shares(i, prob, nodes, entries)

        def finish_by_reciprocal(i):
            for nodes, entries in pieces(i):
                width = entries.stop - entries.start
                ex = keep.tile([P, width], F32, name=f"ex{i}_{nodes.start}")
                nc.scalar.activation(ex[:], shifted[i][:, entries], ACT.Exp)
                ex_sum = keep.tile([P, width // D], F32, name=f"ex_sum{i}_{nodes.start}")
                nc.vector.tensor_reduce(ex_sum[:], by_node(ex[:]), AXIS_X, ALU.add)
                inv_sum = keep.tile([P, width // D], F32, name=f"inv_sum{i}_{nodes.start}")
                nc.vector.reciprocal(inv_sum[:], ex_sum[:])
                prob = keep.tile([P, width], F32, name=f"prob{i}_{nodes.start}")
                nc.vector.tensor_tensor(by_node(prob[:]), by_node(ex[:]), per_node(inv_sum[:]), ALU.mult)
                take_off_shares(i, prob, nodes, entries)

        for step in range(LAST + 2):
            if 0 <= step - 2 < LAST:
                finish_by_log(step - 2)
            if 0 <= step - 1 < LAST:
                negative_log(step - 1)
            if step < LAST:
                shift(step)
                sum_children(step)
            elif step == LAST:
                shift(step)
                finish_by_reciprocal(step)
